import numpy as np
CORES = [0,8,16,24,32,40,48,56,64,72,80,88,96,104,112,120]
N = 16
T = 32
ROUTE = [[[9],[2],[9],[9],[11],[9],[9],[7],[0],[9],[15],[13],[1],[9],[9],[5],[11],[11],[9],[10],[15],[9],[14],[5],[9],[9],[9],[6],[2],[9],[9],[9]],[[10],[9],[9],[14],[8],[9],[3],[15],[9],[3],[5],[1],[9],[0],[9],[9],[9],[9],[1],[14],[11],[9],[15],[9],[9],[6],[14],[6],[9],[5],[7],[9]],[[0],[10],[13],[13],[9],[7],[13],[1],[3],[9],[9],[13],[9],[2],[9],[3],[9],[15],[8],[9],[4],[12],[9],[5],[13],[13],[15],[5],[9],[9],[7],[15]],[[0],[13],[9],[9],[9],[9],[10],[9],[9],[15],[8],[2],[8],[4],[3],[3],[9],[0],[8],[3],[9],[15],[9],[8],[9],[2],[9],[11],[9],[9],[5],[9]],[[9],[0],[9],[9],[9],[1],[3],[9],[9],[9],[6],[10],[7],[13],[7],[9],[4],[9],[1],[11],[5],[9],[1],[9],[15],[13],[10],[9],[9],[12],[15],[13]],[[5],[6],[13],[14],[12],[8],[9],[9],[8],[4],[2],[14],[3],[13],[4],[9],[9],[9],[6],[6],[9],[9],[9],[9],[9],[7],[4],[9],[4],[3],[9],[3]],[[2],[1],[1],[8],[13],[0],[6],[2],[4],[9],[9],[9],[4],[9],[12],[13],[0],[9],[11],[13],[9],[14],[9],[1],[6],[9],[3],[9],[9],[3],[13],[6]],[[6],[8],[3],[4],[9],[2],[9],[10],[3],[4],[13],[5],[7],[9],[3],[4],[9],[1],[14],[5],[8],[9],[9],[10],[9],[15],[3],[12],[0],[9],[2],[9]],[[10],[3],[10],[4],[4],[12],[5],[12],[4],[10],[2],[15],[1],[2],[9],[9],[7],[11],[7],[8],[9],[6],[4],[10],[13],[9],[13],[1],[10],[3],[9],[9]],[[9],[9],[11],[9],[11],[9],[14],[6],[12],[9],[1],[5],[1],[12],[1],[9],[9],[14],[4],[6],[8],[6],[9],[0],[8],[15],[9],[13],[6],[9],[9],[0]],[[3],[8],[9],[7],[9],[9],[6],[5],[6],[1],[6],[9],[9],[9],[9],[13],[15],[2],[7],[9],[4],[9],[9],[9],[4],[14],[15],[1],[5],[9],[15],[0]],[[7],[9],[1],[9],[5],[2],[9],[9],[10],[9],[9],[13],[9],[1],[9],[9],[12],[7],[5],[9],[3],[14],[1],[2],[3],[7],[9],[5],[12],[9],[8],[6]],[[9],[5],[11],[15],[9],[0],[9],[13],[9],[9],[14],[0],[15],[9],[14],[14],[9],[13],[9],[10],[9],[9],[0],[14],[9],[7],[9],[9],[9],[11],[9],[9]],[[9],[3],[9],[9],[7],[4],[14],[9],[9],[9],[9],[7],[9],[13],[8],[5],[12],[12],[13],[9],[12],[9],[9],[2],[2],[9],[5],[9],[15],[12],[9],[11]],[[8],[6],[4],[10],[4],[9],[4],[0],[13],[2],[5],[0],[2],[9],[9],[9],[7],[3],[13],[0],[14],[2],[9],[4],[11],[1],[3],[9],[0],[3],[6],[11]],[[9],[10],[10],[9],[9],[0],[9],[14],[7],[9],[14],[4],[12],[9],[14],[10],[9],[9],[9],[12],[6],[9],[9],[9],[8],[1],[9],[8],[11],[7],[1],[12]]]
CAP = 24
YW = 24
def setup_inputs(rng):
    return {"x": rng.standard_normal((N, 128, T), dtype=np.float32)}
def reference(x):
    y = np.full((N, 128, YW), np.nan, x.dtype)
    fill = [0] * N
    for r in range(N):
        for t in range(T):
            for e in ROUTE[r][t]:
                if fill[e] < CAP:
                    y[e][:, fill[e]] = x[r][:, t]
                fill[e] += 1
    return {"y": y}

@@ -1,0 +1,281 @@
+from concourse.bass import RemoteDMATransfer, DstId
+
+SCRATCH = {
+    "xs": ("sbuf", [128, 32], "float32"),
+    "xh": ("sbuf", [128, 32], "float32"),
+    "land": ("sbuf", [128, 24], "float32"),
+}
+SEMAPHORES = ["loaded", "got", "sent", "arrived", "stored"]
+
+PORT_CORES = (2, 6, 3, 7)
+PLAIN_CORES = (4, 1, 5)
+GOAL = 64
+CACHE = {}
+
+
+def pow2floor(n):
+    p = 1
+    while p * 2 <= n:
+        p *= 2
+    return p
+
+
+def level(m):
+    return 128 // pow2floor(8 // m)
+
+
+def engine_split(n, total, base):
+    e = [pow2floor(total // n)] * n
+    spare = total - sum(e)
+    for i in range(n):
+        if e[i] <= spare:
+            spare -= e[i]
+            e[i] *= 2
+    out, bit = [], base
+    for k in e:
+        out.append((((1 << k) - 1) << bit, k))
+        bit += k
+    return out
+
+
+def kept_runs(route, n, tokens, cap):
+    fill = [0] * n
+    runs = [[] for r in range(n)]
+    for r in range(n):
+        for t in range(tokens):
+            for e in route[r][t]:
+                if fill[e] < cap:
+                    lst = runs[r]
+                    if lst and lst[-1][2] == e and lst[-1][0] + lst[-1][1] == t:
+                        c, w, ee, d = lst[-1]
+                        lst[-1] = (c, w + 1, ee, d)
+                    else:
+                        lst.append((t, 1, e, fill[e]))
+                fill[e] += 1
+    return runs, [min(f, cap) for f in fill]
+
+
+def singles(run):
+    c, w, e, d = run
+    return [(c + i, 1, e, d + i) for i in range(w)]
+
+
+def span_of(runs):
+    return max(c + w for c, w, e, d in runs) - min(c for c, w, e, d in runs)
+
+
+def chunkings(runs, k, free):
+    n = len(runs)
+    caps = [c for c in (1, 2, 4, 8) if c * k >= n]
+    if not caps or k > n:
+        return None
+    cap = caps[0]
+    memo = {}
+
+    def f(i, kk, fr):
+        if kk == 0:
+            return (0, ()) if (i == n and not fr) else None
+        key = (i, kk, fr)
+        if key in memo:
+            return memo[key]
+        best = None
+        for j in range(1, cap + 1):
+            if i + j > n:
+                break
+            for use in ((False, True) if fr else (False,)):
+                rest = f(i + j, kk - 1, fr and not use)
+                if rest is None:
+                    continue
+                cost = max(0 if use else span_of(runs[i:i + j]), rest[0])
+                if best is None or cost < best[0]:
+                    best = (cost, ((j, use),) + rest[1])
+        memo[key] = best
+        return best
+
+    res = f(0, k, free)
+    if res is None:
+        return None
+    chunks, i = [], 0
+    for j, use in res[1]:
+        chunks.append((runs[i:i + j], use))
+        i += j
+    return res[0], max(j for j, use in res[1]), chunks
+
+
+def compositions(limits, total):
+    if not limits:
+        yield ()
+        return
+    for k in range(1, min(limits[0], total) + 1):
+        for rest in compositions(limits[1:], total - k):
+            yield (k,) + rest
+
+
+def plan_group(runs, cores, free):
+    big = sorted({w for c, w, e, d in runs if w > 1})
+    best = None
+    for bits in range(1 << len(big)):
+        cls = {}
+        for run in runs:
+            w = run[1]
+            if w > 1 and (bits >> big.index(w)) & 1:
+                cls.setdefault(1, []).extend(singles(run))
+            else:
+                cls.setdefault(w, []).append(run)
+        ws = sorted(cls)
+        for w in ws:
+            cls[w].sort()
+        ntr = sum(len(cls[w]) for w in ws)
+        for ks in compositions([len(cls[w]) for w in ws], cores):
+            for fw in (ws if free else [None]):
+                chunks, wid, m, ok = [], 0, 1, True
+                for w, k in zip(ws, ks):
+                    res = chunkings(cls[w], k, fw == w)
+                    if res is None:
+                        ok = False
+                        break
+                    wid = max(wid, res[0])
+                    m = max(m, res[1])
+                    chunks.extend(res[2])
+                if not ok:
+                    continue
+                key = (max(level(m), GOAL), ntr, sum(ks), wid)
+                if best is None or key < best[0]:
+                    best = (key, chunks)
+    return best
+
+
+def make_plan(tables, cores):
+    route, tokens, cap = tables["ROUTE"], tables["T"], tables["CAP"]
+    n = len(route)
+    runs, counts = kept_runs(route, n, tokens, cap)
+    cross, same, idle = {}, {}, {}
+    for r in range(n):
+        xr = [u for u in runs[r] if (u[2] ^ r) & 1]
+        sr = [u for u in runs[r] if not (u[2] ^ r) & 1 and u[2] != r]
+        cross[r] = plan_group(xr, len(PORT_CORES), False) if xr else ((GOAL, 0, 0, 0), [])
+        spare = len(PORT_CORES) - len(cross[r][1])
+        same[r] = plan_group(sr, 1 + len(PLAIN_CORES) + spare, True) if sr else ((GOAL, 0, 0, 0), [])
+        idle[r] = spare - max(0, len(same[r][1]) - 1 - len(PLAIN_CORES))
+    abroad = {r: [] for r in range(n)}
+    for r in range(n):
+        while cross[r][0][0] > GOAL:
+            left = [u for ch, fr in cross[r][1] for u in ch]
+            best = None
+            for w, e in sorted({(u[1], u[2]) for u in left}):
+                m = e ^ 1
+                if m == r or idle[m] <= 0:
+                    continue
+                grp = sorted(u for u in left if u[1] == w and u[2] == e)
+                for i in range(max(1, len(grp) - 3)):
+                    take = grp[i:i + 4]
+                    res = plan_group([u for u in left if u not in take], len(PORT_CORES), False)
+                    key = (res[0][0], res[0][1] + len(take), max(res[0][3], span_of(take)))
+                    if best is None or key < best[0]:
+                        best = (key, res, take, m)
+            if best is None or best[0][0] >= cross[r][0][0]:
+                break
+            cross[r] = best[1]
+            abroad[r].append((best[3], best[2]))
+            idle[best[3]] -= 1
+    jobs, helpers = {}, {}
+    for r in range(n):
+        chip0 = cores[r]
+        ports = list(PORT_CORES)
+        hs = []
+        for ch, fr in sorted(cross[r][1], key=lambda cf: -len(cf[0])):
+            k = ports.pop(0)
+            jobs[chip0 + k] = {"rank": r, "runs": list(ch), "home": []}
+            hs.append(chip0 + k)
+        others = list(PLAIN_CORES) + ports
+        for ch, fr in same[r][1]:
+            k = 0 if fr else others.pop(0)
+            jobs[chip0 + k] = {"rank": r, "runs": list(ch), "home": []}
+            if k:
+                hs.append(chip0 + k)
+        helpers[r] = hs
+        idle[r] = [k for k in others if k in PORT_CORES]
+    for r in range(n):
+        for m, take in abroad[r]:
+            c = cores[m] + idle[m].pop(0)
+            jobs[c] = {"rank": r, "runs": list(take), "home": []}
+            helpers[r].insert(0, c)
+    for r in range(n):
+        todo = [u for u in runs[r] if u[2] == r]
+        while todo:
+            u = todo.pop(0)
+            cand = [c for c in helpers[r] if c // 8 == cores[r] // 8 and len(jobs[c]["home"]) < 8
+                    and (jobs[c]["runs"] + jobs[c]["home"])[0][1] == u[1]]
+            if not cand:
+                todo = singles(u) + todo
+                continue
+            c = min(cand, key=lambda c: (span_of(jobs[c]["runs"] + jobs[c]["home"] + [u]), len(jobs[c]["home"]), c))
+            jobs[c]["home"].append(u)
+    width = {}
+    for r in range(n):
+        width[r] = max([span_of(jobs[c]["runs"] + jobs[c]["home"]) for c in helpers[r]] + [1])
+    arrive = [0] * n
+    for c in sorted(jobs):
+        j = jobs[c]
+        r = j["rank"]
+        j["start"] = 0 if c == cores[r] else min(min(u[0] for u in j["runs"] + j["home"]), tokens - width[r])
+        j["masks"] = (engine_split(len(j["runs"]), 8, 0) if j["runs"] else []) + \
+                     (engine_split(len(j["home"]), 8, 8) if j["home"] else [])
+        for u, (mask, k) in zip(j["runs"] + j["home"], j["masks"]):
+            arrive[u[2]] += k
+    return {"jobs": jobs, "helpers": helpers, "counts": counts, "width": width, "arrive": arrive}
+
+
+def rank_program(g, core, T, topo):
+    if "plan" not in CACHE:
+        CACHE["plan"] = make_plan(T.tables, list(T.cores))
+    plan = CACHE["plan"]
+    cores = list(T.cores)
+    rank = T.rank_of(core)
+    job = plan["jobs"].get(core)
+    if rank is None and job is None:
+        return
+
+    def dst_id(c):
+        rid, pid, ring = topo.addr(c)
+        return DstId(rid=rid, pnc=pid)
+
+    def scatter(src_buf):
+        trs, n = [], 0
+        for (c, w, e, d), (mask, k) in zip(job["runs"] + job["home"], job["masks"]):
+            a = c - job["start"]
+            trs.append(RemoteDMATransfer(dst_ids=[dst_id(cores[e])], dma_engine_mask=mask, remote_sem=T.sem.arrived,
+                                         src=src_buf[:, a:a + w], dst=T.land[:, d:d + w]))
+            n += k
+        g.remote_dma_fused(trs, local_sem=T.sem.sent)
+        return n
+
+    if rank is None:
+        r = job["rank"]
+        hs = plan["helpers"][r]
+        k = engine_split(len(hs), 16, 0)[hs.index(core)][1]
+        g.wait_ge(T.sem.got, k)
+        n = scatter(T.xh)
+        g.wait_ge(T.sem.sent, n)
+        return
+
+    g.dma_start(T.xs[:], T.x[:]).then_inc(T.sem.loaded, 16)
+    g.wait_ge(T.sem.loaded, 16)
+    sent = 0
+    hs = plan["helpers"][rank]
+    if hs:
+        wd = plan["width"][rank]
+        trs = []
+        for c, (mask, k) in zip(hs, engine_split(len(hs), 16, 0)):
+            s = plan["jobs"][c]["start"]
+            trs.append(RemoteDMATransfer(dst_ids=[dst_id(c)], dma_engine_mask=mask, remote_sem=T.sem.got,
+                                         src=T.xs[:, s:s + wd], dst=T.xh[:, 0:wd]))
+            sent += k
+        g.remote_dma_fused(trs, local_sem=T.sem.sent)
+    if job is not None:
+        sent += scatter(T.xs)
+    cnt = plan["counts"][rank]
+    g.wait_ge(T.sem.arrived, plan["arrive"][rank])
+    g.dma_start(T.y[:, 0:cnt], T.land[:, 0:cnt]).then_inc(T.sem.stored, 16)
+    g.wait_ge(T.sem.sent, sent)
+    g.wait_ge(T.sem.stored, 16)

@@ -145,6 +145,73 @@ def plan_group(runs, cores, free):
     return best
 
 
+def links_of(chip, low_die, dst_chip):
+    out = []
+    if chip == dst_chip:
+        return out
+    if (chip ^ dst_chip) & 1:
+        out.append(("mate", chip, low_die))
+        chip ^= 1
+    if chip != dst_chip:
+        out.append(("out", chip, low_die))
+        out.append(("in", dst_chip, low_die))
+    return out
+
+
+def balance_dies(todo, chip_of_rank):
+    load = {}
+
+    def add(j, low, sign):
+        for u in j["runs"]:
+            for l in links_of(j["chip"], low, chip_of_rank[u[2]]):
+                load[l] = load.get(l, 0) + sign
+
+    by_chip = {}
+    for j in todo:
+        if j["k"] == 0:
+            add(j, True, 1)
+        else:
+            by_chip.setdefault(j["chip"], []).append(j)
+    for js in by_chip.values():
+        js.sort(key=lambda j: not j["port"])
+        for i, j in enumerate(js):
+            j["low"] = (i % 2 == 1) and i < 6
+            add(j, j["low"], 1)
+    better = True
+    while better:
+        better = False
+        for chip in sorted(by_chip):
+            js = by_chip[chip]
+            cur = [j["low"] for j in js]
+            for j in js:
+                add(j, j["low"], -1)
+            best = None
+            for bits in range(1 << len(js)):
+                pat = [bool((bits >> i) & 1) for i in range(len(js))]
+                if sum(pat) > 3 or len(js) - sum(pat) > 4:
+                    continue
+                if sum(1 for j, p in zip(js, pat) if j["port"] and p) > 2:
+                    continue
+                if sum(1 for j, p in zip(js, pat) if j["port"] and not p) > 2:
+                    continue
+                for j, p in zip(js, pat):
+                    add(j, p, 1)
+                key = (max(load.values()), sum(v ** 3 for v in load.values()), pat != cur)
+                for j, p in zip(js, pat):
+                    add(j, p, -1)
+                if best is None or key < best[0]:
+                    best = (key, pat)
+            if best[1] != cur:
+                better = True
+            for j, p in zip(js, best[1]):
+                j["low"] = p
+                add(j, p, 1)
+    for js in by_chip.values():
+        seats = {True: [2, 3, 1], False: [6, 7, 4, 5]}
+        for j in js:
+            j["k"] = seats[j["low"]].pop(0) if j["port"] else seats[j["low"]].pop()
+
+
 def make_plan(tables, cores):
     route, tokens, cap = tables["ROUTE"], tables["T"], tables["CAP"]
     n = len(route)
@@ -178,28 +245,24 @@ def make_plan(tables, cores):
             cross[r] = best[1]
             abroad[r].append((best[3], best[2]))
             idle[best[3]] -= 1
-    jobs, helpers = {}, {}
+    todo = []
     for r in range(n):
-        chip0 = cores[r]
-        ports = list(PORT_CORES)
-        hs = []
-        for ch, fr in sorted(cross[r][1], key=lambda cf: -len(cf[0])):
-            k = ports.pop(0)
-            jobs[chip0 + k] = {"rank": r, "runs": list(ch), "home": []}
-            hs.append(chip0 + k)
-        others = list(PLAIN_CORES) + ports
+        for ch, fr in cross[r][1]:
+            todo.append({"rank": r, "runs": list(ch), "home": [], "chip": cores[r] // 8, "port": True, "k": None})
         for ch, fr in same[r][1]:
-            k = 0 if fr else others.pop(0)
-            jobs[chip0 + k] = {"rank": r, "runs": list(ch), "home": []}
-            if k:
-                hs.append(chip0 + k)
-        helpers[r] = hs
-        idle[r] = [k for k in others if k in PORT_CORES]
-    for r in range(n):
+            todo.append({"rank": r, "runs": list(ch), "home": [], "chip": cores[r] // 8, "port": False,
+                         "k": 0 if fr else None})
         for m, take in abroad[r]:
-            c = cores[m] + idle[m].pop(0)
-            jobs[c] = {"rank": r, "runs": list(take), "home": []}
-            helpers[r].insert(0, c)
+            todo.append({"rank": r, "runs": list(take), "home": [], "chip": cores[m] // 8, "port": True, "k": None})
+    balance_dies(todo, [c // 8 for c in cores])
+    jobs, helpers = {}, {r: [] for r in range(n)}
+    for j in todo:
+        c = j["chip"] * 8 + j["k"]
+        jobs[c] = j
+        if c != cores[j["rank"]]:
+            helpers[j["rank"]].append((j["chip"] == cores[j["rank"]] // 8, not j["port"], c))
+    for r in range(n):
+        helpers[r] = [c for a, b, c in sorted(helpers[r])]
     for r in range(n):
         todo = [u for u in runs[r] if u[2] == r]
         while todo:
@@ -211,19 +274,28 @@ def make_plan(tables, cores):
                 continue
             c = min(cand, key=lambda c: (span_of(jobs[c]["runs"] + jobs[c]["home"] + [u]), len(jobs[c]["home"]), c))
             jobs[c]["home"].append(u)
-    width = {}
+    first, width, fan = {}, {}, {}
     for r in range(n):
-        width[r] = max([span_of(jobs[c]["runs"] + jobs[c]["home"]) for c in helpers[r]] + [1])
+        hs = helpers[r]
+        served = [u for c in hs for u in jobs[c]["runs"] + jobs[c]["home"]]
+        first[r] = min([u[0] for u in served] + [tokens - 1])
+        width[r] = max([u[0] + u[1] for u in served] + [first[r] + 1]) - first[r]
+        if all(c // 8 == cores[r] // 8 for c in hs):
+            fan[r] = [(0xFFFF, 16, hs)]
+        else:
+            half = (len(hs) + 1) // 2
+            fan[r] = [(0x00FF, 8, hs[:half]), (0xFF00, 8, hs[half:])]
     arrive = [0] * n
     for c in sorted(jobs):
         j = jobs[c]
         r = j["rank"]
-        j["start"] = 0 if c == cores[r] else min(min(u[0] for u in j["runs"] + j["home"]), tokens - width[r])
+        j["start"] = 0 if c == cores[r] else first[r]
         j["masks"] = (engine_split(len(j["runs"]), 8, 0) if j["runs"] else []) + \
                      (engine_split(len(j["home"]), 8, 8) if j["home"] else [])
         for u, (mask, k) in zip(j["runs"] + j["home"], j["masks"]):
             arrive[u[2]] += k
-    return {"jobs": jobs, "helpers": helpers, "counts": counts, "width": width, "arrive": arrive}
+    return {"jobs": jobs, "helpers": helpers, "counts": counts, "first": first, "width": width, "fan": fan,
+            "arrive": arrive}
 
 
 def rank_program(g, core, T, topo):
@@ -251,9 +323,7 @@ def rank_program(g, core, T, topo):
         return n
 
     if rank is None:
-        r = job["rank"]
-        hs = plan["helpers"][r]
-        k = engine_split(len(hs), 16, 0)[hs.index(core)][1]
+        k = [k for mask, k, hs in plan["fan"][job["rank"]] if core in hs][0]
         g.wait_ge(T.sem.got, k)
         n = scatter(T.xh)
         g.wait_ge(T.sem.sent, n)
@@ -262,14 +332,12 @@ def rank_program(g, core, T, topo):
     g.dma_start(T.xs[:], T.x[:]).then_inc(T.sem.loaded, 16)
     g.wait_ge(T.sem.loaded, 16)
     sent = 0
-    hs = plan["helpers"][rank]
-    if hs:
-        wd = plan["width"][rank]
+    if plan["helpers"][rank]:
+        s, wd = plan["first"][rank], plan["width"][rank]
         trs = []
-        for c, (mask, k) in zip(hs, engine_split(len(hs), 16, 0)):
-            s = plan["jobs"][c]["start"]
-            trs.append(RemoteDMATransfer(dst_ids=[dst_id(c)], dma_engine_mask=mask, remote_sem=T.sem.got,
-                                         src=T.xs[:, s:s + wd], dst=T.xh[:, 0:wd]))
+        for mask, k, hs in plan["fan"][rank]:
+            trs.append(RemoteDMATransfer(dst_ids=[dst_id(c) for c in hs], dma_engine_mask=mask, remote_sem=T.sem.got,
+                                         srcs=[T.xs[:, s:s + wd]], dsts=[T.xh[:, 0:wd] for c in hs]))
             sent += k
         g.remote_dma_fused(trs, local_sem=T.sem.sent)
     if job is not None:

@@ -6,10 +6,6 @@ SCRATCH = {
     "land": ("sbuf", [128, 24], "float32"),
 }
 SEMAPHORES = ["loaded", "got", "sent", "arrived", "stored"]
-
-PORT_CORES = (2, 6, 3, 7)
-PLAIN_CORES = (4, 1, 5)
-GOAL = 64
 CACHE = {}
 
 
@@ -18,10 +14,6 @@ def pow2floor(n):
     while p * 2 <= n:
         p *= 2
     return p
-
-
-def level(m):
-    return 128 // pow2floor(8 // m)
 
 
 def engine_split(n, total, base):
@@ -58,91 +50,6 @@ def kept_runs(route, n, tokens, cap):
 def singles(run):
     c, w, e, d = run
     return [(c + i, 1, e, d + i) for i in range(w)]
-
-
-def span_of(runs):
-    return max(c + w for c, w, e, d in runs) - min(c for c, w, e, d in runs)
-
-
-def chunkings(runs, k, free):
-    n = len(runs)
-    caps = [c for c in (1, 2, 4, 8) if c * k >= n]
-    if not caps or k > n:
-        return None
-    cap = caps[0]
-    memo = {}
-
-    def f(i, kk, fr):
-        if kk == 0:
-            return (0, ()) if (i == n and not fr) else None
-        key = (i, kk, fr)
-        if key in memo:
-            return memo[key]
-        best = None
-        for j in range(1, cap + 1):
-            if i + j > n:
-                break
-            for use in ((False, True) if fr else (False,)):
-                rest = f(i + j, kk - 1, fr and not use)
-                if rest is None:
-                    continue
-                cost = max(0 if use else span_of(runs[i:i + j]), rest[0])
-                if best is None or cost < best[0]:
-                    best = (cost, ((j, use),) + rest[1])
-        memo[key] = best
-        return best
-
-    res = f(0, k, free)
-    if res is None:
-        return None
-    chunks, i = [], 0
-    for j, use in res[1]:
-        chunks.append((runs[i:i + j], use))
-        i += j
-    return res[0], max(j for j, use in res[1]), chunks
-
-
-def compositions(limits, total):
-    if not limits:
-        yield ()
-        return
-    for k in range(1, min(limits[0], total) + 1):
-        for rest in compositions(limits[1:], total - k):
-            yield (k,) + rest
-
-
-def plan_group(runs, cores, free):
-    big = sorted({w for c, w, e, d in runs if w > 1})
-    best = None
-    for bits in range(1 << len(big)):
-        cls = {}
-        for run in runs:
-            w = run[1]
-            if w > 1 and (bits >> big.index(w)) & 1:
-                cls.setdefault(1, []).extend(singles(run))
-            else:
-                cls.setdefault(w, []).append(run)
-        ws = sorted(cls)
-        for w in ws:
-            cls[w].sort()
-        ntr = sum(len(cls[w]) for w in ws)
-        for ks in compositions([len(cls[w]) for w in ws], cores):
-            for fw in (ws if free else [None]):
-                chunks, wid, m, ok = [], 0, 1, True
-                for w, k in zip(ws, ks):
-                    res = chunkings(cls[w], k, fw == w)
-                    if res is None:
-                        ok = False
-                        break
-                    wid = max(wid, res[0])
-                    m = max(m, res[1])
-                    chunks.extend(res[2])
-                if not ok:
-                    continue
-                key = (max(level(m), GOAL), ntr, sum(ks), wid)
-                if best is None or key < best[0]:
-                    best = (key, chunks)
-    return best
 
 
 def links_of(chip, low_die, dst_chip):
@@ -216,86 +123,77 @@ def make_plan(tables, cores):
     route, tokens, cap = tables["ROUTE"], tables["T"], tables["CAP"]
     n = len(route)
     runs, counts = kept_runs(route, n, tokens, cap)
-    cross, same, idle = {}, {}, {}
-    for r in range(n):
-        xr = [u for u in runs[r] if (u[2] ^ r) & 1]
-        sr = [u for u in runs[r] if not (u[2] ^ r) & 1 and u[2] != r]
-        cross[r] = plan_group(xr, len(PORT_CORES), False) if xr else ((GOAL, 0, 0, 0), [])
-        spare = len(PORT_CORES) - len(cross[r][1])
-        same[r] = plan_group(sr, 1 + len(PLAIN_CORES) + spare, True) if sr else ((GOAL, 0, 0, 0), [])
-        idle[r] = spare - max(0, len(same[r][1]) - 1 - len(PLAIN_CORES))
-    abroad = {r: [] for r in range(n)}
-    for r in range(n):
-        while cross[r][0][0] > GOAL:
-            left = [u for ch, fr in cross[r][1] for u in ch]
-            best = None
-            for w, e in sorted({(u[1], u[2]) for u in left}):
-                m = e ^ 1
-                if m == r or idle[m] <= 0:
-                    continue
-                grp = sorted(u for u in left if u[1] == w and u[2] == e)
-                for i in range(max(1, len(grp) - 3)):
-                    take = grp[i:i + 4]
-                    res = plan_group([u for u in left if u not in take], len(PORT_CORES), False)
-                    key = (res[0][0], res[0][1] + len(take), max(res[0][3], span_of(take)))
-                    if best is None or key < best[0]:
-                        best = (key, res, take, m)
-            if best is None or best[0][0] >= cross[r][0][0]:
-                break
-            cross[r] = best[1]
-            abroad[r].append((best[3], best[2]))
-            idle[best[3]] -= 1
     todo = []
     for r in range(n):
-        for ch, fr in cross[r][1]:
-            todo.append({"rank": r, "runs": list(ch), "home": [], "chip": cores[r] // 8, "port": True, "k": None})
-        for ch, fr in same[r][1]:
-            todo.append({"rank": r, "runs": list(ch), "home": [], "chip": cores[r] // 8, "port": False,
-                         "k": 0 if fr else None})
-        for m, take in abroad[r]:
-            todo.append({"rank": r, "runs": list(take), "home": [], "chip": cores[m] // 8, "port": True, "k": None})
+        chip = cores[r] // 8
+        cross = sorted(u for u in runs[r] if (u[2] ^ r) & 1)
+        same = sorted(u for u in runs[r] if not (u[2] ^ r) & 1 and u[2] != r)
+        own = sorted((u for u in same if u[1] > 1), key=lambda u: -u[1])[:4]
+        own = [u for u in own if u[1] in sorted({v[1] for v in own})[-2:]]
+        if len({u[1] for u in own}) < 2:
+            own += [u for u in same if u[1] == 1][:4 - len(own)]
+        if own:
+            todo.append({"rank": r, "runs": own, "home": [], "chip": chip, "port": False, "k": 0})
+        rest = [u for u in same if u not in own]
+        full = 4
+        for w in sorted({u[1] for u in cross + rest}):
+            lst = [u for u in cross if u[1] == w] + [u for u in rest if u[1] == w]
+            while lst:
+                take = 4 if (len(lst) > 2 and full > 0) else 2
+                full -= 1 if take == 4 else 0
+                todo.append({"rank": r, "runs": lst[:take], "home": [], "chip": chip, "k": None,
+                             "port": any((u[2] ^ r) & 1 for u in lst[:take])})
+                lst = lst[take:]
+    for r in range(n):
+        chip = cores[r] // 8
+        while sum(1 for j in todo if j["chip"] == chip and j["port"]) > 4:
+            cand = []
+            for j in todo:
+                if j["rank"] == r and j["chip"] == chip and j["port"] and len({u[2] for u in j["runs"]}) == 1:
+                    m = cores[j["runs"][0][2] ^ 1] // 8
+                    if m != chip and sum(1 for i in todo if i["chip"] == m and i["port"]) < 4 \
+                            and sum(1 for i in todo if i["chip"] == m and i["k"] is None) < 7:
+                        cand.append((len(j["runs"]), -j["runs"][0][1], j["runs"][0][0], m, j))
+            cand.sort(key=lambda t: t[:4])
+            cand[0][4]["chip"] = cand[0][3]
     balance_dies(todo, [c // 8 for c in cores])
-    jobs, helpers = {}, {r: [] for r in range(n)}
+    jobs, near, far = {}, {r: [] for r in range(n)}, {r: [] for r in range(n)}
     for j in todo:
         c = j["chip"] * 8 + j["k"]
         jobs[c] = j
-        if c != cores[j["rank"]]:
-            helpers[j["rank"]].append((j["chip"] == cores[j["rank"]] // 8, not j["port"], c))
+        if j["k"]:
+            (near if j["chip"] == cores[j["rank"]] // 8 else far)[j["rank"]].append(c)
     for r in range(n):
-        helpers[r] = [c for a, b, c in sorted(helpers[r])]
-    for r in range(n):
-        todo = [u for u in runs[r] if u[2] == r]
-        while todo:
-            u = todo.pop(0)
-            cand = [c for c in helpers[r] if c // 8 == cores[r] // 8 and len(jobs[c]["home"]) < 8
-                    and (jobs[c]["runs"] + jobs[c]["home"])[0][1] == u[1]]
+        stay = [u for u in runs[r] if u[2] == r]
+        while stay:
+            u = stay.pop(0)
+            cand = [c for c in near[r] if len(jobs[c]["home"]) < 8 and jobs[c]["runs"][0][1] == u[1]]
             if not cand:
-                todo = singles(u) + todo
+                stay = singles(u) + stay
                 continue
-            c = min(cand, key=lambda c: (span_of(jobs[c]["runs"] + jobs[c]["home"] + [u]), len(jobs[c]["home"]), c))
-            jobs[c]["home"].append(u)
+            jobs[min(cand, key=lambda c: (len(jobs[c]["home"]), len(jobs[c]["runs"]), c))]["home"].append(u)
     first, width, fan = {}, {}, {}
     for r in range(n):
-        hs = helpers[r]
-        served = [u for c in hs for u in jobs[c]["runs"] + jobs[c]["home"]]
+        served = [u for c in near[r] + far[r] for u in jobs[c]["runs"] + jobs[c]["home"]]
         first[r] = min([u[0] for u in served] + [tokens - 1])
         width[r] = max([u[0] + u[1] for u in served] + [first[r] + 1]) - first[r]
-        if all(c // 8 == cores[r] // 8 for c in hs):
-            fan[r] = [(0xFFFF, 16, hs)]
-        else:
-            half = (len(hs) + 1) // 2
-            fan[r] = [(0x00FF, 8, hs[:half]), (0xFF00, 8, hs[half:])]
+        order = sorted(near[r], key=lambda c: (-len(jobs[c]["runs"]), c))
+        fan[r] = []
+        if order:
+            fan[r].append([(0xFFFF, 16, order[:4])])
+        if far[r]:
+            fan[r].append([(0x00FF, 8, far[r])] + ([(0xFF00, 8, order[4:])] if order[4:] else []))
+        elif order[4:]:
+            fan[r].append([(0xFFFF, 16, order[4:])])
     arrive = [0] * n
     for c in sorted(jobs):
         j = jobs[c]
-        r = j["rank"]
-        j["start"] = 0 if c == cores[r] else first[r]
+        j["start"] = 0 if j["k"] == 0 else first[j["rank"]]
         j["masks"] = (engine_split(len(j["runs"]), 8, 0) if j["runs"] else []) + \
                      (engine_split(len(j["home"]), 8, 8) if j["home"] else [])
         for u, (mask, k) in zip(j["runs"] + j["home"], j["masks"]):
             arrive[u[2]] += k
-    return {"jobs": jobs, "helpers": helpers, "counts": counts, "first": first, "width": width, "fan": fan,
-            "arrive": arrive}
+    return {"jobs": jobs, "counts": counts, "first": first, "width": width, "fan": fan, "arrive": arrive}
 
 
 def rank_program(g, core, T, topo):
@@ -313,17 +211,22 @@ def rank_program(g, core, T, topo):
         return DstId(rid=rid, pnc=pid)
 
     def scatter(src_buf):
-        trs, n = [], 0
-        for (c, w, e, d), (mask, k) in zip(job["runs"] + job["home"], job["masks"]):
-            a = c - job["start"]
-            trs.append(RemoteDMATransfer(dst_ids=[dst_id(cores[e])], dma_engine_mask=mask, remote_sem=T.sem.arrived,
-                                         src=src_buf[:, a:a + w], dst=T.land[:, d:d + w]))
-            n += k
-        g.remote_dma_fused(trs, local_sem=T.sem.sent)
+        n = 0
+        todo = list(zip(job["runs"] + job["home"], job["masks"]))
+        for width in sorted({u[1] for u, mk in todo}, reverse=True):
+            trs = []
+            for (c, w, e, d), (mask, k) in todo:
+                if w == width:
+                    a = c - job["start"]
+                    trs.append(RemoteDMATransfer(dst_ids=[dst_id(cores[e])], dma_engine_mask=mask,
+                                                 remote_sem=T.sem.arrived,
+                                                 src=src_buf[:, a:a + w], dst=T.land[:, d:d + w]))
+                    n += k
+            g.remote_dma_fused(trs, local_sem=T.sem.sent)
         return n
 
     if rank is None:
-        k = [k for mask, k, hs in plan["fan"][job["rank"]] if core in hs][0]
+        k = [k for call in plan["fan"][job["rank"]] for mask, k, hs in call if core in hs][0]
         g.wait_ge(T.sem.got, k)
         n = scatter(T.xh)
         g.wait_ge(T.sem.sent, n)
@@ -332,10 +235,10 @@ def rank_program(g, core, T, topo):
     g.dma_start(T.xs[:], T.x[:]).then_inc(T.sem.loaded, 16)
     g.wait_ge(T.sem.loaded, 16)
     sent = 0
-    if plan["helpers"][rank]:
-        s, wd = plan["first"][rank], plan["width"][rank]
+    s, wd = plan["first"][rank], plan["width"][rank]
+    for call in plan["fan"][rank]:
         trs = []
-        for mask, k, hs in plan["fan"][rank]:
+        for mask, k, hs in call:
             trs.append(RemoteDMATransfer(dst_ids=[dst_id(c) for c in hs], dma_engine_mask=mask, remote_sem=T.sem.got,
                                          srcs=[T.xs[:, s:s + wd]], dsts=[T.xh[:, 0:wd] for c in hs]))
             sent += k

from concourse.bass import RemoteDMATransfer, DstId

SCRATCH = {
    "xs": ("sbuf", [128, 32], "float32"),
    "xh": ("sbuf", [128, 32], "float32"),
    "land": ("sbuf", [128, 24], "float32"),
}
SEMAPHORES = ["loaded", "got", "sent", "arrived", "stored"]
CACHE = {}


def pow2floor(n):
    p = 1
    while p * 2 <= n:
        p *= 2
    return p


def engine_split(n, total, base):
    e = [pow2floor(total // n)] * n
    spare = total - sum(e)
    for i in range(n):
        if e[i] <= spare:
            spare -= e[i]
            e[i] *= 2
    out, bit = [], base
    for k in e:
        out.append((((1 << k) - 1) << bit, k))
        bit += k
    return out


def kept_runs(route, n, tokens, cap):
    fill = [0] * n
    runs = [[] for r in range(n)]
    for r in range(n):
        for t in range(tokens):
            for e in route[r][t]:
                if fill[e] < cap:
                    lst = runs[r]
                    if lst and lst[-1][2] == e and lst[-1][0] + lst[-1][1] == t:
                        c, w, ee, d = lst[-1]
                        lst[-1] = (c, w + 1, ee, d)
                    else:
                        lst.append((t, 1, e, fill[e]))
                fill[e] += 1
    return runs, [min(f, cap) for f in fill]


def singles(run):
    c, w, e, d = run
    return [(c + i, 1, e, d + i) for i in range(w)]


def links_of(chip, low_die, dst_chip):
    out = []
    if chip == dst_chip:
        return out
    if (chip ^ dst_chip) & 1:
        out.append(("mate", chip, low_die))
        chip ^= 1
    if chip != dst_chip:
        out.append(("out", chip, low_die))
        out.append(("in", dst_chip, low_die))
    return out


def balance_dies(todo, chip_of_rank):
    load = {}

    def add(j, low, sign):
        for u in j["runs"]:
            for l in links_of(j["chip"], low, chip_of_rank[u[2]]):
                load[l] = load.get(l, 0) + sign

    by_chip = {}
    for j in todo:
        if j["k"] == 0:
            add(j, True, 1)
        else:
            by_chip.setdefault(j["chip"], []).append(j)
    for js in by_chip.values():
        js.sort(key=lambda j: not j["port"])
        for i, j in enumerate(js):
            j["low"] = (i % 2 == 1) and i < 6
            add(j, j["low"], 1)
    better = True
    while better:
        better = False
        for chip in sorted(by_chip):
            js = by_chip[chip]
            cur = [j["low"] for j in js]
            for j in js:
                add(j, j["low"], -1)
            best = None
            for bits in range(1 << len(js)):
                pat = [bool((bits >> i) & 1) for i in range(len(js))]
                if sum(pat) > 3 or len(js) - sum(pat) > 4:
                    continue
                if sum(1 for j, p in zip(js, pat) if j["port"] and p) > 2:
                    continue
                if sum(1 for j, p in zip(js, pat) if j["port"] and not p) > 2:
                    continue
                for j, p in zip(js, pat):
                    add(j, p, 1)
                key = (max(load.values()), sum(v ** 3 for v in load.values()), pat != cur)
                for j, p in zip(js, pat):
                    add(j, p, -1)
                if best is None or key < best[0]:
                    best = (key, pat)
            if best[1] != cur:
                better = True
            for j, p in zip(js, best[1]):
                j["low"] = p
                add(j, p, 1)
    for js in by_chip.values():
        seats = {True: [2, 3, 1], False: [6, 7, 4, 5]}
        for j in js:
            j["k"] = seats[j["low"]].pop(0) if j["port"] else seats[j["low"]].pop()


def make_plan(tables, cores):
    route, tokens, cap = tables["ROUTE"], tables["T"], tables["CAP"]
    n = len(route)
    runs, counts = kept_runs(route, n, tokens, cap)
    todo = []
    for r in range(n):
        chip = cores[r] // 8
        cross = sorted(u for u in runs[r] if (u[2] ^ r) & 1)
        same = sorted(u for u in runs[r] if not (u[2] ^ r) & 1 and u[2] != r)
        own = sorted((u for u in same if u[1] > 1), key=lambda u: -u[1])[:4]
        own = [u for u in own if u[1] in sorted({v[1] for v in own})[-2:]]
        if len({u[1] for u in own}) < 2:
            own += [u for u in same if u[1] == 1][:4 - len(own)]
        if own:
            todo.append({"rank": r, "runs": own, "home": [], "chip": chip, "port": False, "k": 0})
        rest = [u for u in same if u not in own]
        full = 4
        for w in sorted({u[1] for u in cross + rest}):
            lst = [u for u in cross if u[1] == w] + [u for u in rest if u[1] == w]
            while lst:
                take = 4 if (len(lst) > 2 and full > 0) else 2
                full -= 1 if take == 4 else 0
                todo.append({"rank": r, "runs": lst[:take], "home": [], "chip": chip, "k": None,
                             "port": any((u[2] ^ r) & 1 for u in lst[:take])})
                lst = lst[take:]
    for r in range(n):
        chip = cores[r] // 8
        while sum(1 for j in todo if j["chip"] == chip and j["port"]) > 4:
            cand = []
            for j in todo:
                if j["rank"] == r and j["chip"] == chip and j["port"] and len({u[2] for u in j["runs"]}) == 1:
                    m = cores[j["runs"][0][2] ^ 1] // 8
                    if m != chip and sum(1 for i in todo if i["chip"] == m and i["port"]) < 4 \
                            and sum(1 for i in todo if i["chip"] == m and i["k"] is None) < 7:
                        cand.append((len(j["runs"]), -j["runs"][0][1], j["runs"][0][0], m, j))
            cand.sort(key=lambda t: t[:4])
            cand[0][4]["chip"] = cand[0][3]
    balance_dies(todo, [c // 8 for c in cores])
    jobs, near, far = {}, {r: [] for r in range(n)}, {r: [] for r in range(n)}
    for j in todo:
        c = j["chip"] * 8 + j["k"]
        jobs[c] = j
        if j["k"]:
            (near if j["chip"] == cores[j["rank"]] // 8 else far)[j["rank"]].append(c)
    for r in range(n):
        stay = [u for u in runs[r] if u[2] == r]
        while stay:
            u = stay.pop(0)
            cand = [c for c in near[r] if len(jobs[c]["home"]) < 8 and jobs[c]["runs"][0][1] == u[1]]
            if not cand:
                stay = singles(u) + stay
                continue
            jobs[min(cand, key=lambda c: (len(jobs[c]["home"]), len(jobs[c]["runs"]), c))]["home"].append(u)
    first, width, fan = {}, {}, {}
    for r in range(n):
        served = [u for c in near[r] + far[r] for u in jobs[c]["runs"] + jobs[c]["home"]]
        first[r] = min([u[0] for u in served] + [tokens - 1])
        width[r] = max([u[0] + u[1] for u in served] + [first[r] + 1]) - first[r]
        order = sorted(near[r], key=lambda c: (-len(jobs[c]["runs"]), c))
        fan[r] = []
        if order:
            fan[r].append([(0xFFFF, 16, order[:4])])
        if far[r]:
            fan[r].append([(0x00FF, 8, far[r])] + ([(0xFF00, 8, order[4:])] if order[4:] else []))
        elif order[4:]:
            fan[r].append([(0xFFFF, 16, order[4:])])
    arrive = [0] * n
    for c in sorted(jobs):
        j = jobs[c]
        j["start"] = 0 if j["k"] == 0 else first[j["rank"]]
        j["masks"] = (engine_split(len(j["runs"]), 8, 0) if j["runs"] else []) + \
                     (engine_split(len(j["home"]), 8, 8) if j["home"] else [])
        for u, (mask, k) in zip(j["runs"] + j["home"], j["masks"]):
            arrive[u[2]] += k
    return {"jobs": jobs, "counts": counts, "first": first, "width": width, "fan": fan, "arrive": arrive}


def rank_program(g, core, T, topo):
    if "plan" not in CACHE:
        CACHE["plan"] = make_plan(T.tables, list(T.cores))
    plan = CACHE["plan"]
    cores = list(T.cores)
    rank = T.rank_of(core)
    job = plan["jobs"].get(core)
    if rank is None and job is None:
        return

    def dst_id(c):
        rid, pid, ring = topo.addr(c)
        return DstId(rid=rid, pnc=pid)

    def scatter(src_buf):
        n = 0
        todo = list(zip(job["runs"] + job["home"], job["masks"]))
        for width in sorted({u[1] for u, mk in todo}, reverse=True):
            trs = []
            for (c, w, e, d), (mask, k) in todo:
                if w == width:
                    a = c - job["start"]
                    trs.append(RemoteDMATransfer(dst_ids=[dst_id(cores[e])], dma_engine_mask=mask,
                                                 remote_sem=T.sem.arrived,
                                                 src=src_buf[:, a:a + w], dst=T.land[:, d:d + w]))
                    n += k
            g.remote_dma_fused(trs, local_sem=T.sem.sent)
        return n

    if rank is None:
        k = [k for call in plan["fan"][job["rank"]] for mask, k, hs in call if core in hs][0]
        g.wait_ge(T.sem.got, k)
        n = scatter(T.xh)
        g.wait_ge(T.sem.sent, n)
        return

    g.dma_start(T.xs[:], T.x[:]).then_inc(T.sem.loaded, 16)
    g.wait_ge(T.sem.loaded, 16)
    sent = 0
    s, wd = plan["first"][rank], plan["width"][rank]
    for call in plan["fan"][rank]:
        trs = []
        for mask, k, hs in call:
            trs.append(RemoteDMATransfer(dst_ids=[dst_id(c) for c in hs], dma_engine_mask=mask, remote_sem=T.sem.got,
                                         srcs=[T.xs[:, s:s + wd]], dsts=[T.xh[:, 0:wd] for c in hs]))
            sent += k
        g.remote_dma_fused(trs, local_sem=T.sem.sent)
    if job is not None:
        sent += scatter(T.xs)
    cnt = plan["counts"][rank]
    g.wait_ge(T.sem.arrived, plan["arrive"][rank])
    g.dma_start(T.y[:, 0:cnt], T.land[:, 0:cnt]).then_inc(T.sem.stored, 16)
    g.wait_ge(T.sem.sent, sent)
    g.wait_ge(T.sem.stored, 16)
